import numpy as np
import ml_dtypes


def mxq(x, axis, fmt="e4m3"):
    dtype, down = {"e4m3": (ml_dtypes.float8_e4m3fn, 7), "e5m2": (ml_dtypes.float8_e5m2, 14)}[fmt]
    v = np.moveaxis(np.asarray(x, np.float32).astype(ml_dtypes.bfloat16).astype(np.float64), axis, -1)
    blocks = v.reshape(v.shape[:-1] + (-1, 32))
    amax = np.abs(blocks).max(-1, keepdims=True)
    byte = np.maximum(np.where(amax > 0, np.frexp(amax)[1] - 1 + 127, 0) - down, 1)
    scale = np.exp2(byte - 127.0)
    codes = (blocks / scale).astype(np.float32).astype(dtype).astype(np.float64)
    return np.moveaxis((codes * scale).reshape(v.shape), -1, axis)


WIDE = False


def mx_kscale(k):
    if not WIDE:
        return np.ones(k)
    levels = np.array([10, -10, 5, -5, 0])
    if k % 512:
        return np.exp2(np.random.permutation(np.resize(levels, k // 32))).repeat(32)
    a = np.empty((k // 512, 16))
    for p in range(k // 512):
        a[p, :8] = np.random.permutation(np.resize(levels, 8))
        for g in range(8):
            far = levels[np.abs(levels - a[p, g]) >= 10]
            a[p, g + 8] = far[np.random.randint(len(far))]
    return np.exp2(a.ravel()).repeat(32)


def f64(x):
    return np.asarray(x).astype(np.float64)


def striped(idx):
    return np.tile(idx.reshape(-1, 16).T, (8, 1)).astype(np.uint16)


def unstriped(offs):
    return offs[:16].T.reshape(-1).astype(np.int64)


def pack_weight(w):
    k, n = w.shape
    w = f64(np.asarray(w, np.float32).astype(ml_dtypes.bfloat16)).reshape(k // 32, 32, n)
    amax = np.abs(w).max(1)
    byte = np.clip(np.where(amax > 0, np.frexp(amax)[1] - 1 + 127 - 7, 1), 1, 254)
    scaled = (w * np.exp2(127.0 - byte)[:, None, :]).reshape(k, n).astype(np.float32)
    words = np.ascontiguousarray(scaled.reshape(k // 512, 128, 4, n).transpose(0, 1, 3, 2)).astype(ml_dtypes.float8_e4m3fn).view(np.uint8)
    return words, np.ascontiguousarray(byte.astype(np.uint8).reshape(k // 512, 16, n))


def unpack_weight(words, scales):
    g, p, n, _ = words.shape
    vals = np.ascontiguousarray(words).view(ml_dtypes.float8_e4m3fn).astype(np.float64) * np.repeat(np.exp2(scales.astype(np.float64) - 127.0), 8, axis=1)[..., None]
    return vals.transpose(0, 1, 3, 2).reshape(g * 512, n)


def silu(v):
    return v / (1.0 + np.exp(-np.maximum(v, -700.0)))


K, T, S, N = 1024, 512, 512, 1024


def setup_inputs():
    n = np.random.standard_normal
    s = mx_kscale(K)[:, None]
    packed = pack_weight(n((K, N)) / np.sqrt(K) / s)
    return {
        "w_words": packed[0],
        "w_scales": packed[1],
        "xT": (n((K, T)) * s).astype(np.float32),
        "b": (0.3 * n((S, 1))).astype(np.float32),
        "offs": striped(np.sort(np.random.permutation(N)[:S])),
    }


def reference(w_words, w_scales, xT, b, offs):
    idx = unstriped(offs)
    wq = unpack_weight(w_words, w_scales)[:, idx]
    return silu((wq.T @ mxq(f64(xT), 0, "e4m3")) + f64(b))

@@ -1,0 +1,137 @@
+from contextlib import ExitStack
+
+import concourse.mybir as mybir
+
+K, T, S, N = 1024, 512, 512, 1024
+FLOPS = 2 * K * S * T
+
+F32 = mybir.dt.float32
+BF16 = mybir.dt.bfloat16
+I32 = mybir.dt.int32
+U32 = mybir.dt.uint32
+U16 = mybir.dt.uint16
+U8 = mybir.dt.uint8
+FP8X4 = mybir.dt.float8_e4m3fn_x4
+SILU = mybir.ActivationFunctionType.Silu
+
+P = 128
+PACK = 4
+K_PASS = P * PACK
+PASSES = K // K_PASS
+HALF = T // 2
+M_TILES = S // P
+
+
+def tile_picked_neuron_lin_silu_srt_p_kernel(tc, w_words, w_scales, xT, b, offs, out):
+    nc = tc.nc
+    with ExitStack() as ctx:
+        keep = ctx.enter_context(tc.tile_pool(name="keep", bufs=1))
+        psum = ctx.enter_context(tc.psum_pool(name="psum", bufs=1))
+
+        offsets = keep.tile([P, S // 16], U16, name="offsets")
+        nc.sync.dma_start(offsets[:], offs)
+
+        scale_table = keep.tile([P, N], U8, name="scale_table", align_bytes=64)
+        nc.vector.memset(scale_table[:].bitcast(I32), 0)
+        for q in range(4):
+            nc.scalar.dma_start(
+                scale_table[32 * q : 32 * q + 4 * PASSES, :].bitcast(I32),
+                w_scales[:, 4 * q : 4 * q + 4, :].bitcast(I32),
+            )
+        bias = keep.tile([P, M_TILES], F32, name="bias")
+        with nc.allow_non_contiguous_dma(reason="one bias a partition"):
+            nc.scalar.dma_start(bias[:], b.rearrange("(m p) one -> p (m one)", p=P))
+        warm = keep.tile([P, 1], F32, name="warm")
+        nc.scalar.activation(warm[:], bias[:, 0:1], SILU)
+
+        word_tables = [keep.tile([P, N], I32, name="word_table%d" % o, align_bytes=64) for o in range(PASSES)]
+        x_first = keep.tile([P, PACK, T], F32, name="x_first", align_bytes=64)
+        x_second = [keep.tile([P, PACK, HALF], F32, name="x_second%d" % h, align_bytes=64) for h in range(2)]
+
+        def load_words(o):
+            nc.sync.dma_start(word_tables[o][:], w_words[o].rearrange("p n t -> p (n t)").bitcast(I32))
+
+        def x_rows(o):
+            return xT[o * K_PASS : (o + 1) * K_PASS, :].rearrange("(p j) t -> p j t", j=PACK)
+
+        load_words(0)
+        nc.sync.dma_start(x_first[:], x_rows(0))
+        load_words(1)
+        for h in range(2):
+            nc.sync.dma_start(x_second[h][:], x_rows(1)[:, :, h * HALF : (h + 1) * HALF])
+
+        picked_scales = keep.tile([P, S], U8, name="picked_scales", align_bytes=64)
+        picked_words = [keep.tile([P, S], U32, name="picked_words%d" % o, align_bytes=64) for o in range(PASSES)]
+
+        def gather_words(o):
+            nc.vector.tensor_copy(picked_words[o][:], word_tables[o][:].bitcast(U32).indirect(offsets[:]))
+
+        grouped = {}
+        codes = {}
+        scales = {}
+        for o in range(PASSES):
+            for h in range(2):
+                grouped[o, h] = keep.tile([P, HALF, PACK], BF16, name="grouped%d%d" % (o, h), align_bytes=64)
+                codes[o, h] = keep.tile([P, HALF], U32, name="codes%d%d" % (o, h), align_bytes=64)
+                scales[o, h] = keep.tile([P, HALF], U8, name="scales%d%d" % (o, h), align_bytes=64)
+
+        def interleave(copy, o, h, t0, t1):
+            raw = x_first[:, :, h * HALF + t0 : h * HALF + t1] if o == 0 else x_second[h][:, :, t0:t1]
+            copy(
+                grouped[o, h][:, t0:t1, :].rearrange("p (c i) j -> p c j i", i=4),
+                raw.rearrange("p j (c i) -> p c j i", i=4),
+            )
+
+        def quantize(o, h):
+            nc.vector.quantize_mx(
+                out=codes[o, h][:].bitcast(FP8X4),
+                scales=scales[o, h][:],
+                in_=grouped[o, h][:].rearrange("p t j -> p (t j)"),
+            )
+
+        acc = {}
+        for h in range(2):
+            for m in range(M_TILES):
+                acc[h, m] = psum.tile([P, HALF], F32, name="acc%d%d" % (h, m))
+
+        def multiply(o, h, m):
+            cols = slice(m * P, (m + 1) * P)
+            nc.tensor.matmul_mx(
+                out=acc[h, m][:],
+                lhsT=picked_words[o][:, cols].bitcast(FP8X4),
+                lhsT_scale=picked_scales[4 * o : P, cols],
+                rhs=codes[o, h][:].bitcast(FP8X4),
+                rhs_scale=scales[o, h][:],
+                start=(o == 0),
+                stop=(o == PASSES - 1),
+            )
+
+        def finish(h, m):
+            result = keep.tile([P, HALF], F32, name="result%d%d" % (h, m))
+            nc.scalar.activation(result[:], acc[h, m][:], SILU, bias=bias[:, m : m + 1])
+            nc.sync.dma_start(out[m * P : (m + 1) * P, h * HALF : (h + 1) * HALF], result[:])
+
+        gather_words(0)
+        nc.vector.tensor_copy(picked_scales[:], scale_table[:].indirect(offsets[:]))
+        interleave(nc.scalar.copy, 0, 1, 0, 192)
+        interleave(nc.vector.tensor_copy, 0, 0, 0, HALF)
+        interleave(nc.vector.tensor_copy, 0, 1, 192, HALF)
+        quantize(0, 0)
+        quantize(0, 1)
+        for h in range(2):
+            for m in range(M_TILES):
+                multiply(0, h, m)
+        gather_words(1)
+        interleave(nc.scalar.copy, 1, 0, 0, 96)
+        interleave(nc.vector.tensor_copy, 1, 0, 96, HALF)
+        quantize(1, 0)
+        for m in range(M_TILES):
+            multiply(1, 0, m)
+        interleave(nc.vector.tensor_copy, 1, 1, 0, HALF)
+        quantize(1, 1)
+        for m in range(M_TILES):
+            finish(0, m)
+        for m in range(M_TILES):
+            multiply(1, 1, m)
+        for m in range(M_TILES):
+            finish(1, m)

@@ -1,6 +1,7 @@
 from contextlib import ExitStack
 
 import concourse.mybir as mybir
+from concourse.masks import make_identity
 
 K, T, S, N = 1024, 512, 512, 1024
 FLOPS = 2 * K * S * T
@@ -18,8 +19,10 @@ P = 128
 PACK = 4
 K_PASS = P * PACK
 PASSES = K // K_PASS
-HALF = T // 2
 M_TILES = S // P
+WIDTHS = [256,128,128]
+STARTS = [sum(WIDTHS[:r]) for r in range(len(WIDTHS))]
+SCALAR_TOKENS = [[192,128],[128,0],[0,0]]
 
 
 def tile_picked_neuron_lin_silu_srt_p_kernel(tc, w_words, w_scales, xT, b, offs, out):
@@ -28,110 +31,143 @@ def tile_picked_neuron_lin_silu_srt_p_kernel(tc, w_words, w_scales, xT, b, offs,
         keep = ctx.enter_context(tc.tile_pool(name="keep", bufs=1))
         psum = ctx.enter_context(tc.psum_pool(name="psum", bufs=1))
 
-        offsets = keep.tile([P, S // 16], U16, name="offsets")
-        nc.sync.dma_start(offsets[:], offs)
-
         scale_table = keep.tile([P, N], U8, name="scale_table", align_bytes=64)
         nc.vector.memset(scale_table[:].bitcast(I32), 0)
-        for q in range(4):
-            nc.scalar.dma_start(
-                scale_table[32 * q : 32 * q + 4 * PASSES, :].bitcast(I32),
-                w_scales[:, 4 * q : 4 * q + 4, :].bitcast(I32),
-            )
-        bias = keep.tile([P, M_TILES], F32, name="bias")
-        with nc.allow_non_contiguous_dma(reason="one bias a partition"):
-            nc.scalar.dma_start(bias[:], b.rearrange("(m p) one -> p (m one)", p=P))
+        bias_rows = keep.tile([P, P], F32, name="bias_rows")
+        nc.gpsimd.memset(bias_rows[:], 0.0)
+        identity = keep.tile([P, P], F32, name="identity")
+        make_identity(nc, identity[:])
         warm = keep.tile([P, 1], F32, name="warm")
-        nc.scalar.activation(warm[:], bias[:, 0:1], SILU)
+        nc.vector.memset(warm[:], 0.0)
+        warmed = keep.tile([P, 1], F32, name="warmed")
+        nc.scalar.activation(warmed[:], warm[:], SILU)
 
+        offsets = keep.tile([P, S // 16], U16, name="offsets")
         word_tables = [keep.tile([P, N], I32, name="word_table%d" % o, align_bytes=64) for o in range(PASSES)]
-        x_first = keep.tile([P, PACK, T], F32, name="x_first", align_bytes=64)
-        x_second = [keep.tile([P, PACK, HALF], F32, name="x_second%d" % h, align_bytes=64) for h in range(2)]
+        raw = {}
+        grouped = {}
+        codes = {}
+        scales = {}
+        for r, width in enumerate(WIDTHS):
+            for o in range(PASSES):
+                raw[r, o] = keep.tile([P, PACK, width], F32, name="raw%d%d" % (r, o), align_bytes=64)
+                grouped[r, o] = keep.tile([P, width, PACK], BF16, name="grouped%d%d" % (r, o), align_bytes=64)
+                codes[r, o] = keep.tile([P, width], U32, name="codes%d%d" % (r, o), align_bytes=64)
+                scales[r, o] = keep.tile([P, width], U8, name="scales%d%d" % (r, o), align_bytes=64)
 
-        def load_words(o):
-            nc.sync.dma_start(word_tables[o][:], w_words[o].rearrange("p n t -> p (n t)").bitcast(I32))
+        def load_words(o, c0=0, c1=N):
+            words = w_words[o].rearrange("p n t -> p (n t)").bitcast(I32)
+            nc.sync.dma_start(word_tables[o][:, c0:c1], words[:, c0:c1])
 
-        def x_rows(o):
-            return xT[o * K_PASS : (o + 1) * K_PASS, :].rearrange("(p j) t -> p j t", j=PACK)
+        def load_scales():
+            for q in range(4):
+                nc.sync.dma_start(
+                    scale_table[32 * q : 32 * q + 4 * PASSES, :].bitcast(I32),
+                    w_scales[:, 4 * q : 4 * q + 4, :].bitcast(I32),
+                )
 
-        load_words(0)
-        nc.sync.dma_start(x_first[:], x_rows(0))
+        def load_x(r, o):
+            rows = xT[o * K_PASS : (o + 1) * K_PASS, :].rearrange("(p j) t -> p j t", j=PACK)
+            nc.sync.dma_start(raw[r, o][:], rows[:, :, STARTS[r] : STARTS[r] + WIDTHS[r]])
+
+        def load_bias():
+            nc.gpsimd.dma_start(bias_rows[0:M_TILES, :], b.rearrange("(m p) one -> m (p one)", p=P))
+
+        nc.sync.dma_start(offsets[:], offs)
+        load_bias()
+        load_words(0, 0, 768)
+        load_words(0, 768, N)
+        load_scales()
+        load_x(0, 0)
         load_words(1)
-        for h in range(2):
-            nc.sync.dma_start(x_second[h][:], x_rows(1)[:, :, h * HALF : (h + 1) * HALF])
+        load_x(0, 1)
+        load_x(1, 0)
+        load_x(1, 1)
+        load_x(2, 0)
+        load_x(2, 1)
 
         picked_scales = keep.tile([P, S], U8, name="picked_scales", align_bytes=64)
         picked_words = [keep.tile([P, S], U32, name="picked_words%d" % o, align_bytes=64) for o in range(PASSES)]
 
-        def gather_words(o):
-            nc.vector.tensor_copy(picked_words[o][:], word_tables[o][:].bitcast(U32).indirect(offsets[:]))
+        def gather_words(o, e0=0, e1=S):
+            window = word_tables[o][:, 0 : N - S + e1].bitcast(U32)
+            nc.vector.tensor_copy(picked_words[o][:, e0:e1], window.indirect(offsets[:, e0 // 16 : e1 // 16]))
 
-        grouped = {}
-        codes = {}
-        scales = {}
-        for o in range(PASSES):
-            for h in range(2):
-                grouped[o, h] = keep.tile([P, HALF, PACK], BF16, name="grouped%d%d" % (o, h), align_bytes=64)
-                codes[o, h] = keep.tile([P, HALF], U32, name="codes%d%d" % (o, h), align_bytes=64)
-                scales[o, h] = keep.tile([P, HALF], U8, name="scales%d%d" % (o, h), align_bytes=64)
+        def gather_scales():
+            nc.vector.tensor_copy(picked_scales[:], scale_table[:].indirect(offsets[:]))
 
-        def interleave(copy, o, h, t0, t1):
-            raw = x_first[:, :, h * HALF + t0 : h * HALF + t1] if o == 0 else x_second[h][:, :, t0:t1]
-            copy(
-                grouped[o, h][:, t0:t1, :].rearrange("p (c i) j -> p c j i", i=4),
-                raw.rearrange("p j (c i) -> p c j i", i=4),
-            )
+        def interleave(r, o):
+            cut = SCALAR_TOKENS[r][o]
+            for copy, t0, t1 in ((nc.scalar.copy, 0, cut), (nc.vector.tensor_copy, cut, WIDTHS[r])):
+                if t1 > t0:
+                    copy(
+                        grouped[r, o][:, t0:t1, :].rearrange("p (c i) j -> p c j i", i=4),
+                        raw[r, o][:, :, t0:t1].rearrange("p j (c i) -> p c j i", i=4),
+                    )
 
-        def quantize(o, h):
+        def quantize(r, o):
             nc.vector.quantize_mx(
-                out=codes[o, h][:].bitcast(FP8X4),
-                scales=scales[o, h][:],
-                in_=grouped[o, h][:].rearrange("p t j -> p (t j)"),
+                out=codes[r, o][:].bitcast(FP8X4),
+                scales=scales[r, o][:],
+                in_=grouped[r, o][:].rearrange("p t j -> p (t j)"),
             )
+
+        bias = keep.tile([P, M_TILES], F32, name="bias")
+
+        def turn_bias():
+            turned = psum.tile([P, P], F32, name="turned", tag="bank7")
+            nc.tensor.transpose(turned[:], bias_rows[:], identity[:])
+            nc.scalar.copy(bias[:], turned[:, 0:M_TILES])
 
         acc = {}
-        for h in range(2):
+
+        def multiply(r, o):
             for m in range(M_TILES):
-                acc[h, m] = psum.tile([P, HALF], F32, name="acc%d%d" % (h, m))
+                if o == 0:
+                    acc[r, m] = psum.tile([P, WIDTHS[r]], F32, name="acc%d%d" % (r, m), tag="bank%d" % (r % 2 * M_TILES + m))
+                cols = slice(m * P, (m + 1) * P)
+                nc.tensor.matmul_mx(
+                    out=acc[r, m][:],
+                    lhsT=picked_words[o][:, cols].bitcast(FP8X4),
+                    lhsT_scale=picked_scales[4 * o : P, cols],
+                    rhs=codes[r, o][:].bitcast(FP8X4),
+                    rhs_scale=scales[r, o][:],
+                    start=(o == 0),
+                    stop=(o == PASSES - 1),
+                )
 
-        def multiply(o, h, m):
-            cols = slice(m * P, (m + 1) * P)
-            nc.tensor.matmul_mx(
-                out=acc[h, m][:],
-                lhsT=picked_words[o][:, cols].bitcast(FP8X4),
-                lhsT_scale=picked_scales[4 * o : P, cols],
-                rhs=codes[o, h][:].bitcast(FP8X4),
-                rhs_scale=scales[o, h][:],
-                start=(o == 0),
-                stop=(o == PASSES - 1),
-            )
+        def finish(r, group):
+            for m0 in range(0, M_TILES, group):
+                result = keep.tile([P, group, WIDTHS[r]], F32, name="result%d%d" % (r, m0))
+                for g in range(group):
+                    m = m0 + g
+                    nc.scalar.activation(result[:, g, :], acc[r, m][:], SILU, bias=bias[:, m : m + 1])
+                rows = out[m0 * P : (m0 + group) * P, STARTS[r] : STARTS[r] + WIDTHS[r]]
+                nc.sync.dma_start(rows.rearrange("(g p) t -> p g t", p=P), result[:])
 
-        def finish(h, m):
-            result = keep.tile([P, HALF], F32, name="result%d%d" % (h, m))
-            nc.scalar.activation(result[:], acc[h, m][:], SILU, bias=bias[:, m : m + 1])
-            nc.sync.dma_start(out[m * P : (m + 1) * P, h * HALF : (h + 1) * HALF], result[:])
-
-        gather_words(0)
-        nc.vector.tensor_copy(picked_scales[:], scale_table[:].indirect(offsets[:]))
-        interleave(nc.scalar.copy, 0, 1, 0, 192)
-        interleave(nc.vector.tensor_copy, 0, 0, 0, HALF)
-        interleave(nc.vector.tensor_copy, 0, 1, 192, HALF)
+        turn_bias()
+        gather_words(0, 0, 256)
+        gather_words(0, 256, S)
+        gather_scales()
+        interleave(0, 0)
         quantize(0, 0)
-        quantize(0, 1)
-        for h in range(2):
-            for m in range(M_TILES):
-                multiply(0, h, m)
+        multiply(0, 0)
         gather_words(1)
-        interleave(nc.scalar.copy, 1, 0, 0, 96)
-        interleave(nc.vector.tensor_copy, 1, 0, 96, HALF)
+        interleave(0, 1)
+        quantize(0, 1)
+        multiply(0, 1)
+        interleave(1, 0)
         quantize(1, 0)
-        for m in range(M_TILES):
-            multiply(1, 0, m)
-        interleave(nc.vector.tensor_copy, 1, 1, 0, HALF)
+        multiply(1, 0)
+        finish(0, 1)
+        interleave(1, 1)
         quantize(1, 1)
-        for m in range(M_TILES):
-            finish(0, m)
-        for m in range(M_TILES):
-            multiply(1, 1, m)
-        for m in range(M_TILES):
-            finish(1, m)
+        multiply(1, 1)
+        interleave(2, 0)
+        quantize(2, 0)
+        finish(1, 2)
+        multiply(2, 0)
+        interleave(2, 1)
+        quantize(2, 1)
+        multiply(2, 1)
+        finish(2, 1)

@@ -66,9 +66,10 @@ def tile_picked_neuron_lin_silu_srt_p_kernel(tc, w_words, w_scales, xT, b, offs,
                     w_scales[:, 4 * q : 4 * q + 4, :].bitcast(I32),
                 )
 
-        def load_x(r, o):
+        def load_x(r, o, t0=0, t1=None):
+            t1 = WIDTHS[r] if t1 is None else t1
             rows = xT[o * K_PASS : (o + 1) * K_PASS, :].rearrange("(p j) t -> p j t", j=PACK)
-            nc.sync.dma_start(raw[r, o][:], rows[:, :, STARTS[r] : STARTS[r] + WIDTHS[r]])
+            nc.sync.dma_start(raw[r, o][:, :, t0:t1], rows[:, :, STARTS[r] + t0 : STARTS[r] + t1])
 
         def load_bias():
             nc.gpsimd.dma_start(bias_rows[0:M_TILES, :], b.rearrange("(m p) one -> m (p one)", p=P))
@@ -80,7 +81,8 @@ def tile_picked_neuron_lin_silu_srt_p_kernel(tc, w_words, w_scales, xT, b, offs,
         load_scales()
         load_x(0, 0)
         load_words(1)
-        load_x(0, 1)
+        load_x(0, 1, 0, 128)
+        load_x(0, 1, 128, 256)
         load_x(1, 0)
         load_x(1, 1)
         load_x(2, 0)
@@ -157,17 +159,17 @@ def tile_picked_neuron_lin_silu_srt_p_kernel(tc, w_words, w_scales, xT, b, offs,
         quantize(0, 1)
         multiply(0, 1)
         interleave(1, 0)
-        quantize(1, 0)
-        multiply(1, 0)
         finish(0, 1)
         interleave(1, 1)
+        quantize(1, 0)
         quantize(1, 1)
+        multiply(1, 0)
         multiply(1, 1)
         interleave(2, 0)
-        quantize(2, 0)
-        finish(1, 2)
-        multiply(2, 0)
         interleave(2, 1)
+        finish(1, 2)
+        quantize(2, 0)
         quantize(2, 1)
+        multiply(2, 0)
         multiply(2, 1)
         finish(2, 1)

from contextlib import ExitStack

import concourse.mybir as mybir
from concourse.masks import make_identity

K, T, S, N = 1024, 512, 512, 1024
FLOPS = 2 * K * S * T

F32 = mybir.dt.float32
BF16 = mybir.dt.bfloat16
I32 = mybir.dt.int32
U32 = mybir.dt.uint32
U16 = mybir.dt.uint16
U8 = mybir.dt.uint8
FP8X4 = mybir.dt.float8_e4m3fn_x4
SILU = mybir.ActivationFunctionType.Silu

P = 128
PACK = 4
K_PASS = P * PACK
PASSES = K // K_PASS
M_TILES = S // P
WIDTHS = [256,128,128]
STARTS = [sum(WIDTHS[:r]) for r in range(len(WIDTHS))]
SCALAR_TOKENS = [[192,128],[128,0],[0,0]]


def tile_picked_neuron_lin_silu_srt_p_kernel(tc, w_words, w_scales, xT, b, offs, out):
    nc = tc.nc
    with ExitStack() as ctx:
        keep = ctx.enter_context(tc.tile_pool(name="keep", bufs=1))
        psum = ctx.enter_context(tc.psum_pool(name="psum", bufs=1))

        scale_table = keep.tile([P, N], U8, name="scale_table", align_bytes=64)
        nc.vector.memset(scale_table[:].bitcast(I32), 0)
        bias_rows = keep.tile([P, P], F32, name="bias_rows")
        nc.gpsimd.memset(bias_rows[:], 0.0)
        identity = keep.tile([P, P], F32, name="identity")
        make_identity(nc, identity[:])
        warm = keep.tile([P, 1], F32, name="warm")
        nc.vector.memset(warm[:], 0.0)
        warmed = keep.tile([P, 1], F32, name="warmed")
        nc.scalar.activation(warmed[:], warm[:], SILU)

        offsets = keep.tile([P, S // 16], U16, name="offsets")
        word_tables = [keep.tile([P, N], I32, name="word_table%d" % o, align_bytes=64) for o in range(PASSES)]
        raw = {}
        grouped = {}
        codes = {}
        scales = {}
        for r, width in enumerate(WIDTHS):
            for o in range(PASSES):
                raw[r, o] = keep.tile([P, PACK, width], F32, name="raw%d%d" % (r, o), align_bytes=64)
                grouped[r, o] = keep.tile([P, width, PACK], BF16, name="grouped%d%d" % (r, o), align_bytes=64)
                codes[r, o] = keep.tile([P, width], U32, name="codes%d%d" % (r, o), align_bytes=64)
                scales[r, o] = keep.tile([P, width], U8, name="scales%d%d" % (r, o), align_bytes=64)

        def load_words(o, c0=0, c1=N):
            words = w_words[o].rearrange("p n t -> p (n t)").bitcast(I32)
            nc.sync.dma_start(word_tables[o][:, c0:c1], words[:, c0:c1])

        def load_scales():
            for q in range(4):
                nc.sync.dma_start(
                    scale_table[32 * q : 32 * q + 4 * PASSES, :].bitcast(I32),
                    w_scales[:, 4 * q : 4 * q + 4, :].bitcast(I32),
                )

        def load_x(r, o, t0=0, t1=None):
            t1 = WIDTHS[r] if t1 is None else t1
            rows = xT[o * K_PASS : (o + 1) * K_PASS, :].rearrange("(p j) t -> p j t", j=PACK)
            nc.sync.dma_start(raw[r, o][:, :, t0:t1], rows[:, :, STARTS[r] + t0 : STARTS[r] + t1])

        def load_bias():
            nc.gpsimd.dma_start(bias_rows[0:M_TILES, :], b.rearrange("(m p) one -> m (p one)", p=P))

        nc.sync.dma_start(offsets[:], offs)
        load_bias()
        load_words(0, 0, 768)
        load_words(0, 768, N)
        load_scales()
        load_x(0, 0)
        load_words(1)
        load_x(0, 1, 0, 128)
        load_x(0, 1, 128, 256)
        load_x(1, 0)
        load_x(1, 1)
        load_x(2, 0)
        load_x(2, 1)

        picked_scales = keep.tile([P, S], U8, name="picked_scales", align_bytes=64)
        picked_words = [keep.tile([P, S], U32, name="picked_words%d" % o, align_bytes=64) for o in range(PASSES)]

        def gather_words(o, e0=0, e1=S):
            window = word_tables[o][:, 0 : N - S + e1].bitcast(U32)
            nc.vector.tensor_copy(picked_words[o][:, e0:e1], window.indirect(offsets[:, e0 // 16 : e1 // 16]))

        def gather_scales():
            nc.vector.tensor_copy(picked_scales[:], scale_table[:].indirect(offsets[:]))

        def interleave(r, o):
            cut = SCALAR_TOKENS[r][o]
            for copy, t0, t1 in ((nc.scalar.copy, 0, cut), (nc.vector.tensor_copy, cut, WIDTHS[r])):
                if t1 > t0:
                    copy(
                        grouped[r, o][:, t0:t1, :].rearrange("p (c i) j -> p c j i", i=4),
                        raw[r, o][:, :, t0:t1].rearrange("p j (c i) -> p c j i", i=4),
                    )

        def quantize(r, o):
            nc.vector.quantize_mx(
                out=codes[r, o][:].bitcast(FP8X4),
                scales=scales[r, o][:],
                in_=grouped[r, o][:].rearrange("p t j -> p (t j)"),
            )

        bias = keep.tile([P, M_TILES], F32, name="bias")

        def turn_bias():
            turned = psum.tile([P, P], F32, name="turned", tag="bank7")
            nc.tensor.transpose(turned[:], bias_rows[:], identity[:])
            nc.scalar.copy(bias[:], turned[:, 0:M_TILES])

        acc = {}

        def multiply(r, o):
            for m in range(M_TILES):
                if o == 0:
                    acc[r, m] = psum.tile([P, WIDTHS[r]], F32, name="acc%d%d" % (r, m), tag="bank%d" % (r % 2 * M_TILES + m))
                cols = slice(m * P, (m + 1) * P)
                nc.tensor.matmul_mx(
                    out=acc[r, m][:],
                    lhsT=picked_words[o][:, cols].bitcast(FP8X4),
                    lhsT_scale=picked_scales[4 * o : P, cols],
                    rhs=codes[r, o][:].bitcast(FP8X4),
                    rhs_scale=scales[r, o][:],
                    start=(o == 0),
                    stop=(o == PASSES - 1),
                )

        def finish(r, group):
            for m0 in range(0, M_TILES, group):
                result = keep.tile([P, group, WIDTHS[r]], F32, name="result%d%d" % (r, m0))
                for g in range(group):
                    m = m0 + g
                    nc.scalar.activation(result[:, g, :], acc[r, m][:], SILU, bias=bias[:, m : m + 1])
                rows = out[m0 * P : (m0 + group) * P, STARTS[r] : STARTS[r] + WIDTHS[r]]
                nc.sync.dma_start(rows.rearrange("(g p) t -> p g t", p=P), result[:])

        turn_bias()
        gather_words(0, 0, 256)
        gather_words(0, 256, S)
        gather_scales()
        interleave(0, 0)
        quantize(0, 0)
        multiply(0, 0)
        gather_words(1)
        interleave(0, 1)
        quantize(0, 1)
        multiply(0, 1)
        interleave(1, 0)
        finish(0, 1)
        interleave(1, 1)
        quantize(1, 0)
        quantize(1, 1)
        multiply(1, 0)
        multiply(1, 1)
        interleave(2, 0)
        interleave(2, 1)
        finish(1, 2)
        quantize(2, 0)
        quantize(2, 1)
        multiply(2, 0)
        multiply(2, 1)
        finish(2, 1)
